import numpy as np
import ml_dtypes


def mxq(x, axis, fmt="e4m3"):
    dtype, down = {"e4m3": (ml_dtypes.float8_e4m3fn, 7), "e5m2": (ml_dtypes.float8_e5m2, 14)}[fmt]
    v = np.moveaxis(np.asarray(x, np.float32).astype(ml_dtypes.bfloat16).astype(np.float64), axis, -1)
    blocks = v.reshape(v.shape[:-1] + (-1, 32))
    amax = np.abs(blocks).max(-1, keepdims=True)
    byte = np.maximum(np.where(amax > 0, np.frexp(amax)[1] - 1 + 127, 0) - down, 1)
    scale = np.exp2(byte - 127.0)
    codes = (blocks / scale).astype(np.float32).astype(dtype).astype(np.float64)
    return np.moveaxis((codes * scale).reshape(v.shape), -1, axis)


WIDE = False


def mx_kscale(k, group=512):
    if not WIDE:
        return np.ones(k)
    levels = np.array([10, -10, 5, -5, 0])
    if group != 512:
        return np.exp2(np.random.permutation(np.resize(levels, k // group))).repeat(group)
    if k % 512:
        return np.exp2(np.random.permutation(np.resize(levels, k // 32))).repeat(32)
    a = np.empty((k // 512, 16))
    for p in range(k // 512):
        a[p, :8] = np.random.permutation(np.resize(levels, 8))
        for g in range(8):
            far = levels[np.abs(levels - a[p, g]) >= 10]
            a[p, g + 8] = far[np.random.randint(len(far))]
    return np.exp2(a.ravel()).repeat(32)


def f64(x):
    return np.asarray(x).astype(np.float64)


def sigmoid(v):
    return 1.0 / (1.0 + np.exp(-v))


G, D, M, O, N = 2, 256, 256, 256, 512


def sgn(shape):
    return np.random.uniform(0.5, 2.0, shape) * np.where(np.random.standard_normal(shape) < 0, -1.0, 1.0)


def setup_inputs():
    n = np.random.standard_normal
    s_d = mx_kscale(D, 0)
    s_m = mx_kscale(M, 0)
    return {
        "x": (n((G, D, N)) * s_d[:, None]).astype(np.float32),
        "w1": (n((G, D, M)) / np.sqrt(D) / s_d[:, None]).astype(np.float32),
        "w2": (n((G, D, M)) / np.sqrt(D) / s_d[:, None]).astype(np.float32),
        "th": (np.random.uniform(0.5, 1.5, (G, M, 1))).astype(np.float32),
        "hs": (sgn((G, M, 1)) * s_m[:, None]).astype(np.float32),
        "wo2": (n((G, M, O)) / np.sqrt(M) / s_m[:, None]).astype(np.float32),
        "ob": (0.5 * n((G, O, 1))).astype(np.float32),
        "osc": (np.random.uniform(0.5, 2.0, (G, O, 1))).astype(np.float32),
    }


def reference(x, w1, w2, th, hs, wo2, ob, osc):
    w1q = mxq(f64(w1), 1, "e4m3")
    xq = mxq(f64(x), 1, "e4m3")
    z1 = w1q.transpose(0, 2, 1) @ xq
    w2q = mxq(f64(w2), 1, "e4m3")
    z2 = w2q.transpose(0, 2, 1) @ xq
    mg = np.sqrt(np.square(z1) + np.square(z2) + 0.05)
    h = mg * sigmoid(mg - f64(th))
    hh = h * f64(hs)
    wo2q = mxq(f64(wo2), 1, "e4m3")
    hhq = mxq(hh, 1, "e4m3")
    y0 = wo2q.transpose(0, 2, 1) @ hhq
    y = np.tanh(y0 + f64(ob)) * f64(osc)
    return y

@@ -1,0 +1,210 @@
+from contextlib import ExitStack
+
+import concourse.mybir as mybir
+
+G, D, M, O, N = 2, 256, 256, 256, 512
+FLOPS = 2 * G * N * (2 * D * M + M * O)
+
+F32 = mybir.dt.float32
+BF16 = mybir.dt.bfloat16
+U32 = mybir.dt.uint32
+U8 = mybir.dt.uint8
+FP8X4 = mybir.dt.float8_e4m3fn_x4
+ACT = mybir.ActivationFunctionType
+ALU = mybir.AluOpType
+
+P = 128
+R = 64
+PACK = 4
+HALF = 256
+COLS = 128
+FLOOR = 0.05
+
+
+def tile_rows_fmagnitude_kernel(tc, x, w1, w2, th, hs, wo2, ob, osc, out):
+    nc = tc.nc
+    with ExitStack() as ctx:
+        sb = ctx.enter_context(tc.tile_pool(name="sb", bufs=1))
+        ps = ctx.enter_context(tc.psum_pool(name="ps", bufs=1))
+        ctx.enter_context(tc.manual_schedule())
+
+        def rows(g):
+            return slice(R * g, R * g + R)
+
+        def load(name, src, width):
+            raw = sb.tile([P, PACK, width], F32, name=name, align_bytes=64)
+            nc.sync.dma_start(out=raw[:], in_=src)
+            return raw
+
+        by_word = "g (p j) c -> (g p) j c"
+        xv = x.rearrange(by_word, j=PACK)
+        x_raw0 = load("x_raw0", xv[:, :, 0:HALF], HALF)
+        w1_raw = load("w1_raw", w1.rearrange(by_word, j=PACK), M)
+        w2_raw = load("w2_raw", w2.rearrange(by_word, j=PACK), M)
+        x_raw1 = load("x_raw1", xv[:, :, HALF:N], HALF)
+        wo_raw = load("wo_raw", wo2.rearrange(by_word, j=PACK), O)
+        th_sb = sb.tile([P, PACK], F32, name="th_sb")
+        nc.sync.dma_start(out=th_sb[:], in_=th.rearrange("g (p j) c -> (g p) (j c)", j=PACK))
+        hs_sb = sb.tile([P, PACK], F32, name="hs_sb")
+        nc.sync.dma_start(out=hs_sb[:], in_=hs.rearrange("g (p j) c -> (g p) (j c)", j=PACK))
+        ob_sb = sb.tile([P, 4, 1], F32, name="ob_sb")
+        osc_sb = sb.tile([P, 4, 1], F32, name="osc_sb")
+        with nc.allow_non_contiguous_dma(reason="one value a partition"):
+            nc.sync.dma_start(out=ob_sb[:], in_=ob.rearrange("g (t q) c -> q (g t) c", q=P))
+            nc.sync.dma_start(out=osc_sb[:], in_=osc.rearrange("g (t q) c -> q (g t) c", q=P))
+
+        one = sb.tile([P, 1], F32, name="one")
+        nc.gpsimd.memset(one[:], 1.0)
+        warm = sb.tile([P, 1], F32, name="warm")
+        nc.scalar.activation(out=warm[:], in_=one[:], func=ACT.Sqrt)
+        neg_th = sb.tile([P, PACK], F32, name="neg_th")
+        nc.gpsimd.tensor_scalar(out=neg_th[:], in0=th_sb[:], scalar1=-1.0, scalar2=0.0, op0=ALU.mult, op1=ALU.add)
+
+        def words(name, width):
+            return sb.tile([P, width * PACK], BF16, name=name, align_bytes=64)
+
+        def interleave(copy, dst, raw, first, last):
+            copy(
+                out=dst[:, PACK * first : PACK * last].rearrange("p (c i j) -> p c j i", i=2, j=PACK),
+                in_=raw[:, :, first:last].rearrange("p j (c i) -> p c j i", i=2),
+            )
+
+        def quantize(name, src, width):
+            codes = sb.tile([P, width], U32, name=name + "_codes", align_bytes=64)
+            scales = sb.tile([P, width], U8, name=name + "_scales", align_bytes=64)
+            nc.vector.quantize_mx(out=codes[:].bitcast(FP8X4), scales=scales[:], in_=src)
+            return codes, scales
+
+        def product(dst, g, weights, wcols, moving, mcols):
+            nc.tensor.matmul_mx(
+                out=dst,
+                lhsT=weights[0][rows(g), wcols].bitcast(FP8X4),
+                lhsT_scale=weights[1][rows(g), wcols],
+                rhs=moving[0][rows(g), mcols].bitcast(FP8X4),
+                rhs_scale=moving[1][rows(g), mcols],
+                start=True,
+                stop=True,
+            )
+
+        def first_layer(h, w, wq, xq):
+            banks = [ps.tile([P, 2, HALF], F32, name="z", tag="bank%d%d" % (g, 2 * h + w)) for g in range(G)]
+            for g in range(G):
+                for t in range(2):
+                    for e in range(2):
+                        product(banks[g][:, t, COLS * e : COLS * e + COLS], g, wq, slice(P * t, P * t + P),
+                                xq, slice(COLS * e, COLS * e + COLS))
+            return banks
+
+        def square(name, bank):
+            sq = sb.tile([P, 2, HALF], F32, name=name, align_bytes=64)
+            nc.scalar.activation(out=sq[:], in_=bank[:], func=ACT.Square)
+            return sq
+
+        x_il0 = words("x_il0", HALF)
+        interleave(nc.vector.tensor_copy, x_il0, x_raw0, 0, HALF)
+        xq0 = quantize("xq0", x_il0[:], HALF)
+        w1_il = words("w1_il", M)
+        interleave(nc.vector.tensor_copy, w1_il, w1_raw, 0, 176)
+        interleave(nc.scalar.copy, w1_il, w1_raw, 176, M)
+        w1q = quantize("w1q", w1_il[:], M)
+        z10 = first_layer(0, 0, w1q, xq0)
+        w2_il = words("w2_il", M)
+        interleave(nc.vector.tensor_copy, w2_il, w2_raw, 0, M)
+        w2q = quantize("w2q", w2_il[:], M)
+        z20 = first_layer(0, 1, w2q, xq0)
+        x_il1 = words("x_il1", HALF)
+        interleave(nc.vector.tensor_copy, x_il1, x_raw1, 0, HALF)
+        xq1 = quantize("xq1", x_il1[:], HALF)
+        z11 = first_layer(1, 0, w1q, xq1)
+        z21 = first_layer(1, 1, w2q, xq1)
+
+        mg = [sb.tile([P, PACK, HALF], F32, name="mg%d" % h, align_bytes=64) for h in range(2)]
+
+        def add(name, a, b):
+            total = sb.tile([P, 2, HALF], F32, name=name, align_bytes=64)
+            nc.vector.tensor_tensor(out=total[:], in0=a[:], in1=b[:], op=ALU.add)
+            return total
+
+        def root(h, g, total):
+            wide = sb.tile([P, 2, HALF], F32, name="wide%d%d" % (h, g), align_bytes=64)
+            nc.scalar.activation(out=wide[:], in_=total[:], func=ACT.Sqrt, bias=FLOOR)
+            for t in range(2):
+                first = R * g + 32 * t
+                nc.sync.dma_start(out=mg[h][first : first + 32], in_=wide[:, t, :])
+
+        def scale(h):
+            u = sb.tile([P, PACK, HALF], F32, name="u%d" % h, align_bytes=64)
+            for j in range(PACK):
+                nc.vector.tensor_scalar(out=u[:, j, :], in0=mg[h][:, j, :], scalar1=hs_sb[:, j : j + 1], scalar2=None,
+                                        op0=ALU.mult)
+            return u
+
+        a00 = square("a00", z10[0])
+        a01 = square("a01", z10[1])
+        b00 = square("b00", z20[0])
+        s00 = add("s00", a00, b00)
+        b01 = square("b01", z20[1])
+        s01 = add("s01", a01, b01)
+        root(0, 0, s00)
+        a10 = square("a10", z11[0])
+        root(0, 1, s01)
+        a11 = square("a11", z11[1])
+        b10 = square("b10", z21[0])
+        s10 = add("s10", a10, b10)
+        b11 = square("b11", z21[1])
+        s11 = add("s11", a11, b11)
+        root(1, 0, s10)
+        root(1, 1, s11)
+
+        wo_il = words("wo_il", O)
+        interleave(nc.vector.tensor_copy, wo_il, wo_raw, 0, O)
+        scaled = [scale(0)]
+        woq = quantize("woq", wo_il[:], O)
+
+        quarters = N // COLS
+        hh = []
+        hq = []
+
+        def gate(q):
+            h, cols = q // 2, slice(COLS * (q % 2), COLS * (q % 2) + COLS)
+            sig = sb.tile([P, PACK, COLS], F32, name="sig%d" % q, align_bytes=64)
+            for j in range(PACK):
+                nc.scalar.activation(out=sig[:, j, :], in_=mg[h][:, j, cols], func=ACT.Sigmoid, bias=neg_th[:, j : j + 1])
+            hidden = words("hh%d" % q, COLS)
+            nc.vector.tensor_tensor(
+                out=hidden[:].rearrange("p (c i j) -> p c j i", i=2, j=PACK),
+                in0=scaled[h][:, :, cols].rearrange("p j (c i) -> p c j i", i=2),
+                in1=sig[:].rearrange("p j (c i) -> p c j i", i=2),
+                op=ALU.mult,
+            )
+            hh.append(hidden)
+
+        def second_layer(q):
+            moving = quantize("hq%d" % q, hh[q][:], COLS)
+            banks = [ps.tile([P, 2, COLS], F32, name="y", tag="bank%d%d" % (g, q)) for g in range(G)]
+            for t in range(2):
+                for g in range(G):
+                    product(banks[g][:, t, :], g, woq, slice(P * t, P * t + P), moving, slice(0, COLS))
+            hq.append(banks)
+
+        out_v = out.rearrange("g (t q) n -> q (g t) n", q=P)
+
+        def finish(q):
+            bent = sb.tile([P, 4, COLS], F32, name="bent%d" % q, align_bytes=64)
+            res = sb.tile([P, 4, COLS], F32, name="res%d" % q, align_bytes=64)
+            for g in range(G):
+                for t in range(2):
+                    k = 2 * g + t
+                    nc.scalar.activation(out=bent[:, k, :], in_=hq[q][g][:, t, :], func=ACT.Tanh, bias=ob_sb[:, k, :])
+                    nc.vector.tensor_scalar(out=res[:, k, :], in0=bent[:, k, :], scalar1=osc_sb[:, k, :], scalar2=None,
+                                            op0=ALU.mult)
+            nc.sync.dma_start(out=out_v[:, :, COLS * q : COLS * q + COLS], in_=res[:])
+
+        gate(0)
+        scaled.append(scale(1))
+        for q in range(1, quarters):
+            gate(q)
+            second_layer(q - 1)
+        second_layer(quarters - 1)
+        for q in range(quarters):
+            finish(q)

@@ -40,171 +40,209 @@ def tile_rows_fmagnitude_kernel(tc, x, w1, w2, th, hs, wo2, ob, osc, out):
         xv = x.rearrange(by_word, j=PACK)
         x_raw0 = load("x_raw0", xv[:, :, 0:HALF], HALF)
         w1_raw = load("w1_raw", w1.rearrange(by_word, j=PACK), M)
+
+        one = sb.tile([P, 1], F32, name="one")
+        nc.vector.memset(one[:], 1.0)
+        runs = sb.tile([P, 2, 4, 32], F32, name="runs", align_bytes=64)
+        nc.vector.memset(runs[:], 0.0)
+        th_sb = sb.tile([P, PACK], F32, name="th_sb")
+        nc.scalar.dma_start(out=th_sb[:], in_=th.rearrange("g (p j) c -> (g p) (j c)", j=PACK))
+        hs_sb = sb.tile([P, PACK], F32, name="hs_sb")
+        nc.scalar.dma_start(out=hs_sb[:], in_=hs.rearrange("g (p j) c -> (g p) (j c)", j=PACK))
+        by_run = "g (t b i) c -> b (g t) (i c)"
+        nc.scalar.dma_start(out=runs[0:P:32, 0], in_=ob.rearrange(by_run, t=2, b=4))
+        nc.scalar.dma_start(out=runs[0:P:32, 1], in_=osc.rearrange(by_run, t=2, b=4))
+        warm = sb.tile([P, 1], F32, name="warm")
+        nc.scalar.activation(out=warm[:], in_=one[:], func=ACT.Sqrt)
+
         w2_raw = load("w2_raw", w2.rearrange(by_word, j=PACK), M)
         x_raw1 = load("x_raw1", xv[:, :, HALF:N], HALF)
         wo_raw = load("wo_raw", wo2.rearrange(by_word, j=PACK), O)
-        th_sb = sb.tile([P, PACK], F32, name="th_sb")
-        nc.sync.dma_start(out=th_sb[:], in_=th.rearrange("g (p j) c -> (g p) (j c)", j=PACK))
-        hs_sb = sb.tile([P, PACK], F32, name="hs_sb")
-        nc.sync.dma_start(out=hs_sb[:], in_=hs.rearrange("g (p j) c -> (g p) (j c)", j=PACK))
-        ob_sb = sb.tile([P, 4, 1], F32, name="ob_sb")
-        osc_sb = sb.tile([P, 4, 1], F32, name="osc_sb")
-        with nc.allow_non_contiguous_dma(reason="one value a partition"):
-            nc.sync.dma_start(out=ob_sb[:], in_=ob.rearrange("g (t q) c -> q (g t) c", q=P))
-            nc.sync.dma_start(out=osc_sb[:], in_=osc.rearrange("g (t q) c -> q (g t) c", q=P))
-
-        one = sb.tile([P, 1], F32, name="one")
-        nc.gpsimd.memset(one[:], 1.0)
-        warm = sb.tile([P, 1], F32, name="warm")
-        nc.scalar.activation(out=warm[:], in_=one[:], func=ACT.Sqrt)
-        neg_th = sb.tile([P, PACK], F32, name="neg_th")
-        nc.gpsimd.tensor_scalar(out=neg_th[:], in0=th_sb[:], scalar1=-1.0, scalar2=0.0, op0=ALU.mult, op1=ALU.add)
 
         def words(name, width):
             return sb.tile([P, width * PACK], BF16, name=name, align_bytes=64)
 
-        def interleave(copy, dst, raw, first, last):
+        def interleave(copy, name, raw, k):
+            dst = words(name, COLS)
             copy(
-                out=dst[:, PACK * first : PACK * last].rearrange("p (c i j) -> p c j i", i=2, j=PACK),
-                in_=raw[:, :, first:last].rearrange("p j (c i) -> p c j i", i=2),
+                out=dst[:].rearrange("p (c i j) -> p c j i", i=2, j=PACK),
+                in_=raw[:, :, COLS * k : COLS * k + COLS].rearrange("p j (c i) -> p c j i", i=2),
             )
+            return dst
 
-        def quantize(name, src, width):
-            codes = sb.tile([P, width], U32, name=name + "_codes", align_bytes=64)
-            scales = sb.tile([P, width], U8, name=name + "_scales", align_bytes=64)
-            nc.vector.quantize_mx(out=codes[:].bitcast(FP8X4), scales=scales[:], in_=src)
+        def quantize(name, src):
+            codes = sb.tile([P, COLS], U32, name=name + "_codes", align_bytes=64)
+            scales = sb.tile([P, COLS], U8, name=name + "_scales", align_bytes=64)
+            nc.vector.quantize_mx(out=codes[:].bitcast(FP8X4), scales=scales[:], in_=src[:])
             return codes, scales
 
-        def product(dst, g, weights, wcols, moving, mcols):
+        def prepare(name, raw, second_copy):
+            first = interleave(nc.vector.tensor_copy, name + "_il0", raw, 0)
+            second = interleave(second_copy, name + "_il1", raw, 1)
+            return [quantize(name + "0", first), quantize(name + "1", second)]
+
+        def product(dst, g, weights, moving):
             nc.tensor.matmul_mx(
                 out=dst,
-                lhsT=weights[0][rows(g), wcols].bitcast(FP8X4),
-                lhsT_scale=weights[1][rows(g), wcols],
-                rhs=moving[0][rows(g), mcols].bitcast(FP8X4),
-                rhs_scale=moving[1][rows(g), mcols],
+                lhsT=weights[0][rows(g)].bitcast(FP8X4),
+                lhsT_scale=weights[1][rows(g)],
+                rhs=moving[0][rows(g)].bitcast(FP8X4),
+                rhs_scale=moving[1][rows(g)],
                 start=True,
                 stop=True,
             )
 
-        def first_layer(h, w, wq, xq):
-            banks = [ps.tile([P, 2, HALF], F32, name="z", tag="bank%d%d" % (g, 2 * h + w)) for g in range(G)]
-            for g in range(G):
-                for t in range(2):
-                    for e in range(2):
-                        product(banks[g][:, t, COLS * e : COLS * e + COLS], g, wq, slice(P * t, P * t + P),
-                                xq, slice(COLS * e, COLS * e + COLS))
+        def half_products(w, wq, xq):
+            banks = [ps.tile([P, 2, HALF], F32, name="z", tag="bank%d%d" % (g, w)) for g in range(G)]
+            for t, order in ((0, ((0, 0), (1, 0), (0, 1), (1, 1))), (1, ((0, 0), (0, 1), (1, 0), (1, 1)))):
+                for g, e in order:
+                    product(banks[g][:, t, COLS * e : COLS * e + COLS], g, wq[t], xq[e])
             return banks
 
-        def square(name, bank):
-            sq = sb.tile([P, 2, HALF], F32, name=name, align_bytes=64)
-            nc.scalar.activation(out=sq[:], in_=bank[:], func=ACT.Square)
-            return sq
+        def quarter_products(q, moving):
+            banks = [ps.tile([P, 2, 2, COLS], F32, name="z", tag="bank%d%d" % (g, q)) for g in range(G)]
+            for w, wq in enumerate((w1q, w2q)):
+                for t in range(2):
+                    for g in range(G):
+                        product(banks[g][:, w, t, :], g, wq[t], moving)
+            return banks
 
-        x_il0 = words("x_il0", HALF)
-        interleave(nc.vector.tensor_copy, x_il0, x_raw0, 0, HALF)
-        xq0 = quantize("xq0", x_il0[:], HALF)
-        w1_il = words("w1_il", M)
-        interleave(nc.vector.tensor_copy, w1_il, w1_raw, 0, 176)
-        interleave(nc.scalar.copy, w1_il, w1_raw, 176, M)
-        w1q = quantize("w1q", w1_il[:], M)
-        z10 = first_layer(0, 0, w1q, xq0)
-        w2_il = words("w2_il", M)
-        interleave(nc.vector.tensor_copy, w2_il, w2_raw, 0, M)
-        w2q = quantize("w2q", w2_il[:], M)
-        z20 = first_layer(0, 1, w2q, xq0)
-        x_il1 = words("x_il1", HALF)
-        interleave(nc.vector.tensor_copy, x_il1, x_raw1, 0, HALF)
-        xq1 = quantize("xq1", x_il1[:], HALF)
-        z11 = first_layer(1, 0, w1q, xq1)
-        z21 = first_layer(1, 1, w2q, xq1)
+        def square(dst, bank):
+            nc.scalar.activation(out=dst, in_=bank[:], func=ACT.Square)
 
-        mg = [sb.tile([P, PACK, HALF], F32, name="mg%d" % h, align_bytes=64) for h in range(2)]
-
-        def add(name, a, b):
-            total = sb.tile([P, 2, HALF], F32, name=name, align_bytes=64)
-            nc.vector.tensor_tensor(out=total[:], in0=a[:], in1=b[:], op=ALU.add)
+        def add(name, shape, a, b):
+            total = sb.tile(shape, F32, name=name, align_bytes=64)
+            nc.vector.tensor_tensor(out=total[:], in0=a, in1=b, op=ALU.add)
             return total
 
-        def root(h, g, total):
-            wide = sb.tile([P, 2, HALF], F32, name="wide%d%d" % (h, g), align_bytes=64)
+        def root(name, total, shape):
+            wide = sb.tile(shape, F32, name=name, align_bytes=64)
             nc.scalar.activation(out=wide[:], in_=total[:], func=ACT.Sqrt, bias=FLOOR)
-            for t in range(2):
-                first = R * g + 32 * t
-                nc.sync.dma_start(out=mg[h][first : first + 32], in_=wide[:, t, :])
+            return wide
 
-        def scale(h):
-            u = sb.tile([P, PACK, HALF], F32, name="u%d" % h, align_bytes=64)
+        def send_home(home, g, t, src):
+            first = R * g + 32 * t
+            nc.sync.dma_start(out=home[first : first + 32], in_=src)
+
+        def scale(name, home, width):
+            u = sb.tile([P, PACK, width], F32, name=name, align_bytes=64)
             for j in range(PACK):
-                nc.vector.tensor_scalar(out=u[:, j, :], in0=mg[h][:, j, :], scalar1=hs_sb[:, j : j + 1], scalar2=None,
+                nc.vector.tensor_scalar(out=u[:, j, :], in0=home[:, j, :], scalar1=hs_sb[:, j : j + 1], scalar2=None,
                                         op0=ALU.mult)
-            return u
+            for first in range(0, width, COLS):
+                scaled.append(u[:, :, first : first + COLS])
 
-        a00 = square("a00", z10[0])
-        a01 = square("a01", z10[1])
-        b00 = square("b00", z20[0])
-        s00 = add("s00", a00, b00)
-        b01 = square("b01", z20[1])
-        s01 = add("s01", a01, b01)
-        root(0, 0, s00)
-        a10 = square("a10", z11[0])
-        root(0, 1, s01)
-        a11 = square("a11", z11[1])
-        b10 = square("b10", z21[0])
-        s10 = add("s10", a10, b10)
-        b11 = square("b11", z21[1])
-        s11 = add("s11", a11, b11)
-        root(1, 0, s10)
-        root(1, 1, s11)
+        xq = prepare("x0", x_raw0, nc.vector.tensor_copy)
+        w1q = prepare("w1", w1_raw, nc.scalar.copy)
+        z1 = half_products(0, w1q, xq)
+        w2q = prepare("w2", w2_raw, nc.vector.tensor_copy)
+        z2 = half_products(1, w2q, xq)
+        xq1 = prepare("x1", x_raw1, nc.vector.tensor_copy)
+        zq2 = quarter_products(2, xq1[0])
+        zq3 = quarter_products(3, xq1[1])
 
-        wo_il = words("wo_il", O)
-        interleave(nc.vector.tensor_copy, wo_il, wo_raw, 0, O)
-        scaled = [scale(0)]
-        woq = quantize("woq", wo_il[:], O)
+        mg_half = sb.tile([P, PACK, HALF], F32, name="mg_half", align_bytes=64)
+        mg2 = sb.tile([P, PACK, COLS], F32, name="mg2", align_bytes=64)
+        mg3 = sb.tile([P, PACK, COLS], F32, name="mg3", align_bytes=64)
+        mg = [mg_half[:, :, 0:COLS], mg_half[:, :, COLS:HALF], mg2[:], mg3[:]]
+        scaled = []
+
+        sq1 = sb.tile([P, G, 2, HALF], F32, name="sq1", align_bytes=64)
+        sq2 = sb.tile([P, G, 2, HALF], F32, name="sq2", align_bytes=64)
+        sqq2 = sb.tile([P, G, 2, 2 * COLS], F32, name="sqq2", align_bytes=64)
+        sqq3 = sb.tile([P, G, 2, 2 * COLS], F32, name="sqq3", align_bytes=64)
+        flat = "p w t n -> p w (t n)"
+
+        def half_root(g, total):
+            wide = root("wide%d" % g, total, [P, 2, HALF])
+            for t in range(2):
+                send_home(mg_half, g, t, wide[:, t, :])
+
+        def quarter_root(q, home, total):
+            wide = root("wideq%d" % q, total, [P, G, 2 * COLS])
+            for t in range(2):
+                for g in range(G):
+                    send_home(home, g, t, wide[:, g, COLS * t : COLS * t + COLS])
+
+        square(sq1[:, 0], z1[0])
+        square(sq1[:, 1], z1[1])
+        square(sq2[:, 0], z2[0])
+        s0 = add("s0", [P, 2, HALF], sq1[:, 0], sq2[:, 0])
+        square(sq2[:, 1], z2[1])
+        s1 = add("s1", [P, 2, HALF], sq1[:, 1], sq2[:, 1])
+        half_root(0, s0)
+        plain = sb.tile([P, 2, 2 * COLS], F32, name="plain", align_bytes=64)
+        nc.vector.tensor_copy(out=plain[:], in_=zq2[1][:].rearrange(flat))
+        nc.scalar.activation(out=sqq2[:, 0], in_=zq2[0][:].rearrange(flat), func=ACT.Square)
+        wo_il0 = interleave(nc.vector.tensor_copy, "wo_il0", wo_raw, 0)
+        nc.vector.tensor_tensor(out=sqq2[:, 1], in0=zq2[1][:].rearrange(flat), in1=plain[:], op=ALU.mult)
+        half_root(1, s1)
+        wo_il1 = interleave(nc.vector.tensor_copy, "wo_il1", wo_raw, 1)
+        s2 = add("s2", [P, G, 2 * COLS], sqq2[:, :, 0, :], sqq2[:, :, 1, :])
+        for g in range(G):
+            nc.scalar.activation(out=sqq3[:, g], in_=zq3[g][:].rearrange(flat), func=ACT.Square)
+        s3 = add("s3", [P, G, 2 * COLS], sqq3[:, :, 0, :], sqq3[:, :, 1, :])
+        quarter_root(2, mg2, s2)
+        quarter_root(3, mg3, s3)
+
+        neg_th = sb.tile([P, PACK], F32, name="neg_th")
+        nc.vector.tensor_scalar(out=neg_th[:], in0=th_sb[:], scalar1=-1.0, scalar2=None, op0=ALU.mult)
+        columns = sb.tile([P, 2, 4, 32], F32, name="columns", align_bytes=64)
+        nc.vector.transpose(out=columns[:].rearrange("p a k i -> p (a k i)"), in_=runs[:].rearrange("p a k i -> p (a k i)"))
+        woq = [quantize("wo0", wo_il0), quantize("wo1", wo_il1)]
+        scale("u_half", mg_half, HALF)
 
         quarters = N // COLS
         hh = []
         hq = []
 
         def gate(q):
-            h, cols = q // 2, slice(COLS * (q % 2), COLS * (q % 2) + COLS)
             sig = sb.tile([P, PACK, COLS], F32, name="sig%d" % q, align_bytes=64)
             for j in range(PACK):
-                nc.scalar.activation(out=sig[:, j, :], in_=mg[h][:, j, cols], func=ACT.Sigmoid, bias=neg_th[:, j : j + 1])
+                nc.scalar.activation(out=sig[:, j, :], in_=mg[q][:, j, :], func=ACT.Sigmoid, bias=neg_th[:, j : j + 1])
             hidden = words("hh%d" % q, COLS)
             nc.vector.tensor_tensor(
                 out=hidden[:].rearrange("p (c i j) -> p c j i", i=2, j=PACK),
-                in0=scaled[h][:, :, cols].rearrange("p j (c i) -> p c j i", i=2),
+                in0=scaled[q].rearrange("p j (c i) -> p c j i", i=2),
                 in1=sig[:].rearrange("p j (c i) -> p c j i", i=2),
                 op=ALU.mult,
             )
             hh.append(hidden)
 
         def second_layer(q):
-            moving = quantize("hq%d" % q, hh[q][:], COLS)
+            moving = quantize("hq%d" % q, hh[q])
             banks = [ps.tile([P, 2, COLS], F32, name="y", tag="bank%d%d" % (g, q)) for g in range(G)]
-            for t in range(2):
-                for g in range(G):
-                    product(banks[g][:, t, :], g, woq, slice(P * t, P * t + P), moving, slice(0, COLS))
+            for g in range(G):
+                for t in range(2):
+                    product(banks[g][:, t, :], g, woq[t], moving)
             hq.append(banks)
 
         out_v = out.rearrange("g (t q) n -> q (g t) n", q=P)
 
-        def finish(q):
+        def finish(q, stores):
             bent = sb.tile([P, 4, COLS], F32, name="bent%d" % q, align_bytes=64)
             res = sb.tile([P, 4, COLS], F32, name="res%d" % q, align_bytes=64)
-            for g in range(G):
-                for t in range(2):
-                    k = 2 * g + t
-                    nc.scalar.activation(out=bent[:, k, :], in_=hq[q][g][:, t, :], func=ACT.Tanh, bias=ob_sb[:, k, :])
-                    nc.vector.tensor_scalar(out=res[:, k, :], in0=bent[:, k, :], scalar1=osc_sb[:, k, :], scalar2=None,
-                                            op0=ALU.mult)
-            nc.sync.dma_start(out=out_v[:, :, COLS * q : COLS * q + COLS], in_=res[:])
+            step = 4 // stores
+            for k in range(4):
+                nc.scalar.activation(out=bent[:, k, :], in_=hq[q][k // 2][:, k % 2, :], func=ACT.Tanh,
+                                     bias=columns[:, 0, k, 0:1])
+                nc.vector.tensor_scalar(out=res[:, k, :], in0=bent[:, k, :], scalar1=columns[:, 1, k, 0:1], scalar2=None,
+                                        op0=ALU.mult)
+                if (k + 1) % step == 0:
+                    nc.sync.dma_start(out=out_v[:, k + 1 - step : k + 1, COLS * q : COLS * q + COLS],
+                                      in_=res[:, k + 1 - step : k + 1, :])
 
         gate(0)
-        scaled.append(scale(1))
-        for q in range(1, quarters):
-            gate(q)
-            second_layer(q - 1)
-        second_layer(quarters - 1)
-        for q in range(quarters):
-            finish(q)
+        second_layer(0)
+        gate(1)
+        scale("u2", mg2, COLS)
+        second_layer(1)
+        gate(2)
+        scale("u3", mg3, COLS)
+        second_layer(2)
+        gate(3)
+        finish(0, 1)
+        second_layer(3)
+        finish(1, 1)
+        finish(2, 1)
+        finish(3, 2)

@@ -62,13 +62,19 @@ def tile_rows_fmagnitude_kernel(tc, x, w1, w2, th, hs, wo2, ob, osc, out):
         def words(name, width):
             return sb.tile([P, width * PACK], BF16, name=name, align_bytes=64)
 
-        def interleave(copy, name, raw, k):
+        def interleave(copy, name, columns_in):
             dst = words(name, COLS)
             copy(
-                out=dst[:].rearrange("p (c i j) -> p c j i", i=2, j=PACK),
-                in_=raw[:, :, COLS * k : COLS * k + COLS].rearrange("p j (c i) -> p c j i", i=2),
+                out=dst[:].rearrange("p (c i j) -> p c j i", i=4, j=PACK),
+                in_=columns_in.rearrange("p j (c i) -> p c j i", i=4),
             )
             return dst
+
+        def halves(raw):
+            return raw[:, :, 0:COLS], raw[:, :, COLS : 2 * COLS]
+
+        def dealt(raw):
+            return raw[:, :, 0:M:2], raw[:, :, 1:M:2]
 
         def quantize(name, src):
             codes = sb.tile([P, COLS], U32, name=name + "_codes", align_bytes=64)
@@ -76,9 +82,9 @@ def tile_rows_fmagnitude_kernel(tc, x, w1, w2, th, hs, wo2, ob, osc, out):
             nc.vector.quantize_mx(out=codes[:].bitcast(FP8X4), scales=scales[:], in_=src[:])
             return codes, scales
 
-        def prepare(name, raw, second_copy):
-            first = interleave(nc.vector.tensor_copy, name + "_il0", raw, 0)
-            second = interleave(second_copy, name + "_il1", raw, 1)
+        def prepare(name, parts, second_copy):
+            first = interleave(nc.vector.tensor_copy, name + "_il0", parts[0])
+            second = interleave(second_copy, name + "_il1", parts[1])
             return [quantize(name + "0", first), quantize(name + "1", second)]
 
         def product(dst, g, weights, moving):
@@ -101,9 +107,9 @@ def tile_rows_fmagnitude_kernel(tc, x, w1, w2, th, hs, wo2, ob, osc, out):
 
         def quarter_products(q, moving):
             banks = [ps.tile([P, 2, 2, COLS], F32, name="z", tag="bank%d%d" % (g, q)) for g in range(G)]
-            for w, wq in enumerate((w1q, w2q)):
-                for t in range(2):
-                    for g in range(G):
+            for g in range(G):
+                for w, wq in enumerate((w1q, w2q)):
+                    for t in range(2):
                         product(banks[g][:, w, t, :], g, wq[t], moving)
             return banks
 
@@ -120,24 +126,12 @@ def tile_rows_fmagnitude_kernel(tc, x, w1, w2, th, hs, wo2, ob, osc, out):
             nc.scalar.activation(out=wide[:], in_=total[:], func=ACT.Sqrt, bias=FLOOR)
             return wide
 
-        def send_home(home, g, t, src):
-            first = R * g + 32 * t
-            nc.sync.dma_start(out=home[first : first + 32], in_=src)
-
-        def scale(name, home, width):
-            u = sb.tile([P, PACK, width], F32, name=name, align_bytes=64)
-            for j in range(PACK):
-                nc.vector.tensor_scalar(out=u[:, j, :], in0=home[:, j, :], scalar1=hs_sb[:, j : j + 1], scalar2=None,
-                                        op0=ALU.mult)
-            for first in range(0, width, COLS):
-                scaled.append(u[:, :, first : first + COLS])
-
-        xq = prepare("x0", x_raw0, nc.vector.tensor_copy)
-        w1q = prepare("w1", w1_raw, nc.scalar.copy)
+        xq = prepare("x0", halves(x_raw0), nc.vector.tensor_copy)
+        w1q = prepare("w1", dealt(w1_raw), nc.scalar.copy)
         z1 = half_products(0, w1q, xq)
-        w2q = prepare("w2", w2_raw, nc.vector.tensor_copy)
+        w2q = prepare("w2", dealt(w2_raw), nc.vector.tensor_copy)
         z2 = half_products(1, w2q, xq)
-        xq1 = prepare("x1", x_raw1, nc.vector.tensor_copy)
+        xq1 = prepare("x1", halves(x_raw1), nc.vector.tensor_copy)
         zq2 = quarter_products(2, xq1[0])
         zq3 = quarter_products(3, xq1[1])
 
@@ -145,7 +139,6 @@ def tile_rows_fmagnitude_kernel(tc, x, w1, w2, th, hs, wo2, ob, osc, out):
         mg2 = sb.tile([P, PACK, COLS], F32, name="mg2", align_bytes=64)
         mg3 = sb.tile([P, PACK, COLS], F32, name="mg3", align_bytes=64)
         mg = [mg_half[:, :, 0:COLS], mg_half[:, :, COLS:HALF], mg2[:], mg3[:]]
-        scaled = []
 
         sq1 = sb.tile([P, G, 2, HALF], F32, name="sq1", align_bytes=64)
         sq2 = sb.tile([P, G, 2, HALF], F32, name="sq2", align_bytes=64)
@@ -155,59 +148,55 @@ def tile_rows_fmagnitude_kernel(tc, x, w1, w2, th, hs, wo2, ob, osc, out):
 
         def half_root(g, total):
             wide = root("wide%d" % g, total, [P, 2, HALF])
-            for t in range(2):
-                send_home(mg_half, g, t, wide[:, t, :])
+            nc.sync.dma_start(out=mg_half[rows(g)], in_=wide[:])
 
         def quarter_root(q, home, total):
             wide = root("wideq%d" % q, total, [P, G, 2 * COLS])
-            for t in range(2):
-                for g in range(G):
-                    send_home(home, g, t, wide[:, g, COLS * t : COLS * t + COLS])
+            for g in range(G):
+                nc.sync.dma_start(out=home[rows(g)], in_=wide[:, g, :])
 
         square(sq1[:, 0], z1[0])
         square(sq1[:, 1], z1[1])
         square(sq2[:, 0], z2[0])
         s0 = add("s0", [P, 2, HALF], sq1[:, 0], sq2[:, 0])
         square(sq2[:, 1], z2[1])
-        s1 = add("s1", [P, 2, HALF], sq1[:, 1], sq2[:, 1])
-        half_root(0, s0)
+        nc.scalar.activation(out=sqq2[:, 0], in_=zq2[0][:].rearrange(flat), func=ACT.Square)
         plain = sb.tile([P, 2, 2 * COLS], F32, name="plain", align_bytes=64)
         nc.vector.tensor_copy(out=plain[:], in_=zq2[1][:].rearrange(flat))
-        nc.scalar.activation(out=sqq2[:, 0], in_=zq2[0][:].rearrange(flat), func=ACT.Square)
-        wo_il0 = interleave(nc.vector.tensor_copy, "wo_il0", wo_raw, 0)
+        s1 = add("s1", [P, 2, HALF], sq1[:, 1], sq2[:, 1])
+        half_root(0, s0)
         nc.vector.tensor_tensor(out=sqq2[:, 1], in0=zq2[1][:].rearrange(flat), in1=plain[:], op=ALU.mult)
-        half_root(1, s1)
-        wo_il1 = interleave(nc.vector.tensor_copy, "wo_il1", wo_raw, 1)
-        s2 = add("s2", [P, G, 2 * COLS], sqq2[:, :, 0, :], sqq2[:, :, 1, :])
         for g in range(G):
             nc.scalar.activation(out=sqq3[:, g], in_=zq3[g][:].rearrange(flat), func=ACT.Square)
+        half_root(1, s1)
+        s2 = add("s2", [P, G, 2 * COLS], sqq2[:, :, 0, :], sqq2[:, :, 1, :])
         s3 = add("s3", [P, G, 2 * COLS], sqq3[:, :, 0, :], sqq3[:, :, 1, :])
         quarter_root(2, mg2, s2)
         quarter_root(3, mg3, s3)
+        warm_gate = sb.tile([P, 1], F32, name="warm_gate")
+        nc.scalar.activation(out=warm_gate[:], in_=one[:], func=ACT.Sigmoid)
 
         neg_th = sb.tile([P, PACK], F32, name="neg_th")
         nc.vector.tensor_scalar(out=neg_th[:], in0=th_sb[:], scalar1=-1.0, scalar2=None, op0=ALU.mult)
         columns = sb.tile([P, 2, 4, 32], F32, name="columns", align_bytes=64)
         nc.vector.transpose(out=columns[:].rearrange("p a k i -> p (a k i)"), in_=runs[:].rearrange("p a k i -> p (a k i)"))
-        woq = [quantize("wo0", wo_il0), quantize("wo1", wo_il1)]
-        scale("u_half", mg_half, HALF)
+        woq = prepare("wo", halves(wo_raw), nc.vector.tensor_copy)
 
         quarters = N // COLS
-        hh = []
-        hq = []
+        sig = [sb.tile([P, PACK, COLS], F32, name="sig%d" % q, align_bytes=64) for q in range(quarters)]
+        hidden = [sb.tile([P, PACK, COLS], BF16, name="hidden%d" % q, align_bytes=64) for q in range(quarters)]
+        bent = [sb.tile([P, 4, COLS], F32, name="bent%d" % q, align_bytes=64) for q in range(quarters)]
+        res = [sb.tile([P, 4, COLS], F32, name="res%d" % q, align_bytes=64) for q in range(quarters)]
+        hh = {}
+        y = {}
 
-        def gate(q):
-            sig = sb.tile([P, PACK, COLS], F32, name="sig%d" % q, align_bytes=64)
-            for j in range(PACK):
-                nc.scalar.activation(out=sig[:, j, :], in_=mg[q][:, j, :], func=ACT.Sigmoid, bias=neg_th[:, j : j + 1])
-            hidden = words("hh%d" % q, COLS)
-            nc.vector.tensor_tensor(
-                out=hidden[:].rearrange("p (c i j) -> p c j i", i=2, j=PACK),
-                in0=scaled[q].rearrange("p j (c i) -> p c j i", i=2),
-                in1=sig[:].rearrange("p j (c i) -> p c j i", i=2),
-                op=ALU.mult,
-            )
-            hh.append(hidden)
+        def gate(q, j):
+            nc.scalar.activation(out=sig[q][:, j, :], in_=mg[q][:, j, :], func=ACT.Sigmoid, bias=neg_th[:, j : j + 1])
+            nc.vector.scalar_tensor_tensor(out=hidden[q][:, j, :], in0=mg[q][:, j, :], scalar=hs_sb[:, j : j + 1],
+                                           in1=sig[q][:, j, :], op0=ALU.mult, op1=ALU.mult)
+
+        def pack(q):
+            hh.setdefault(q, interleave(nc.vector.tensor_copy, "hh%d" % q, hidden[q][:]))
 
         def second_layer(q):
             moving = quantize("hq%d" % q, hh[q])
@@ -215,34 +204,49 @@ def tile_rows_fmagnitude_kernel(tc, x, w1, w2, th, hs, wo2, ob, osc, out):
             for g in range(G):
                 for t in range(2):
                     product(banks[g][:, t, :], g, woq[t], moving)
-            hq.append(banks)
+            y.setdefault(q, banks)
 
         out_v = out.rearrange("g (t q) n -> q (g t) n", q=P)
 
-        def finish(q, stores):
-            bent = sb.tile([P, 4, COLS], F32, name="bent%d" % q, align_bytes=64)
-            res = sb.tile([P, 4, COLS], F32, name="res%d" % q, align_bytes=64)
-            step = 4 // stores
+        def bend(q):
             for k in range(4):
-                nc.scalar.activation(out=bent[:, k, :], in_=hq[q][k // 2][:, k % 2, :], func=ACT.Tanh,
+                nc.scalar.activation(out=bent[q][:, k, :], in_=y[q][k // 2][:, k % 2, :], func=ACT.Tanh,
                                      bias=columns[:, 0, k, 0:1])
-                nc.vector.tensor_scalar(out=res[:, k, :], in0=bent[:, k, :], scalar1=columns[:, 1, k, 0:1], scalar2=None,
-                                        op0=ALU.mult)
-                if (k + 1) % step == 0:
-                    nc.sync.dma_start(out=out_v[:, k + 1 - step : k + 1, COLS * q : COLS * q + COLS],
-                                      in_=res[:, k + 1 - step : k + 1, :])
 
-        gate(0)
-        second_layer(0)
-        gate(1)
-        scale("u2", mg2, COLS)
-        second_layer(1)
-        gate(2)
-        scale("u3", mg3, COLS)
-        second_layer(2)
-        gate(3)
-        finish(0, 1)
+        def factor(q, k):
+            nc.vector.tensor_scalar(out=res[q][:, k, :], in0=bent[q][:, k, :], scalar1=columns[:, 1, k, 0:1], scalar2=None,
+                                    op0=ALU.mult)
+
+        def store(q, first, last):
+            nc.sync.dma_start(out=out_v[:, first:last, COLS * q : COLS * q + COLS], in_=res[q][:, first:last, :])
+
+        for j in range(PACK):
+            gate(0, j)
+        for q in range(1, quarters):
+            gate(q, 0)
+            pack(q - 1)
+            gate(q, 1)
+            gate(q, 2)
+            second_layer(q - 1)
+            gate(q, 3)
+        bend(0)
+        for k in range(4):
+            nc.scalar.activation(out=res[0][:, k, :], in_=bent[0][:, k, :], func=ACT.Copy, scale=columns[:, 1, k, 0:1])
+        store(0, 0, 4)
+        bend(1)
+        factor(1, 0)
+        pack(3)
+        factor(1, 1)
+        factor(1, 2)
         second_layer(3)
-        finish(1, 1)
-        finish(2, 1)
-        finish(3, 2)
+        factor(1, 3)
+        store(1, 0, 4)
+        bend(2)
+        for k in range(4):
+            factor(2, k)
+        store(2, 0, 4)
+        bend(3)
+        for g in range(G):
+            factor(3, 2 * g)
+            factor(3, 2 * g + 1)
+            store(3, 2 * g, 2 * g + 2)

@@ -45,19 +45,20 @@ def tile_rows_fmagnitude_kernel(tc, x, w1, w2, th, hs, wo2, ob, osc, out):
         nc.vector.memset(one[:], 1.0)
         runs = sb.tile([P, 2, 4, 32], F32, name="runs", align_bytes=64)
         nc.vector.memset(runs[:], 0.0)
-        th_sb = sb.tile([P, PACK], F32, name="th_sb")
-        nc.scalar.dma_start(out=th_sb[:], in_=th.rearrange("g (p j) c -> (g p) (j c)", j=PACK))
-        hs_sb = sb.tile([P, PACK], F32, name="hs_sb")
-        nc.scalar.dma_start(out=hs_sb[:], in_=hs.rearrange("g (p j) c -> (g p) (j c)", j=PACK))
-        by_run = "g (t b i) c -> b (g t) (i c)"
-        nc.scalar.dma_start(out=runs[0:P:32, 0], in_=ob.rearrange(by_run, t=2, b=4))
-        nc.scalar.dma_start(out=runs[0:P:32, 1], in_=osc.rearrange(by_run, t=2, b=4))
         warm = sb.tile([P, 1], F32, name="warm")
         nc.scalar.activation(out=warm[:], in_=one[:], func=ACT.Sqrt)
 
         w2_raw = load("w2_raw", w2.rearrange(by_word, j=PACK), M)
         x_raw1 = load("x_raw1", xv[:, :, HALF:N], HALF)
         wo_raw = load("wo_raw", wo2.rearrange(by_word, j=PACK), O)
+
+        th_sb = sb.tile([P, PACK], F32, name="th_sb")
+        nc.sync.dma_start(out=th_sb[:], in_=th.rearrange("g (p j) c -> (g p) (j c)", j=PACK))
+        hs_sb = sb.tile([P, PACK], F32, name="hs_sb")
+        nc.sync.dma_start(out=hs_sb[:], in_=hs.rearrange("g (p j) c -> (g p) (j c)", j=PACK))
+        by_run = "g (t b i) c -> b (g t) (i c)"
+        nc.sync.dma_start(out=runs[0:P:32, 0], in_=ob.rearrange(by_run, t=2, b=4))
+        nc.sync.dma_start(out=runs[0:P:32, 1], in_=osc.rearrange(by_run, t=2, b=4))
 
         def words(name, width):
             return sb.tile([P, width * PACK], BF16, name=name, align_bytes=64)
@@ -135,10 +136,8 @@ def tile_rows_fmagnitude_kernel(tc, x, w1, w2, th, hs, wo2, ob, osc, out):
         zq2 = quarter_products(2, xq1[0])
         zq3 = quarter_products(3, xq1[1])
 
-        mg_half = sb.tile([P, PACK, HALF], F32, name="mg_half", align_bytes=64)
-        mg2 = sb.tile([P, PACK, COLS], F32, name="mg2", align_bytes=64)
-        mg3 = sb.tile([P, PACK, COLS], F32, name="mg3", align_bytes=64)
-        mg = [mg_half[:, :, 0:COLS], mg_half[:, :, COLS:HALF], mg2[:], mg3[:]]
+        quarters = N // COLS
+        mg = [sb.tile([P, PACK, COLS], F32, name="mg%d" % q, align_bytes=64) for q in range(quarters)]
 
         sq1 = sb.tile([P, G, 2, HALF], F32, name="sq1", align_bytes=64)
         sq2 = sb.tile([P, G, 2, HALF], F32, name="sq2", align_bytes=64)
@@ -146,14 +145,12 @@ def tile_rows_fmagnitude_kernel(tc, x, w1, w2, th, hs, wo2, ob, osc, out):
         sqq3 = sb.tile([P, G, 2, 2 * COLS], F32, name="sqq3", align_bytes=64)
         flat = "p w t n -> p w (t n)"
 
-        def half_root(g, total):
-            wide = root("wide%d" % g, total, [P, 2, HALF])
-            nc.sync.dma_start(out=mg_half[rows(g)], in_=wide[:])
+        def send_half(queue, g, wide):
+            for q in range(2):
+                queue.dma_start(out=mg[q][rows(g)], in_=wide[:, :, COLS * q : COLS * q + COLS])
 
-        def quarter_root(q, home, total):
-            wide = root("wideq%d" % q, total, [P, G, 2 * COLS])
-            for g in range(G):
-                nc.sync.dma_start(out=home[rows(g)], in_=wide[:, g, :])
+        def send_quarter(queue, q, g, wide):
+            queue.dma_start(out=mg[q][rows(g)], in_=wide[:, g, :])
 
         square(sq1[:, 0], z1[0])
         square(sq1[:, 1], z1[1])
@@ -164,15 +161,20 @@ def tile_rows_fmagnitude_kernel(tc, x, w1, w2, th, hs, wo2, ob, osc, out):
         plain = sb.tile([P, 2, 2 * COLS], F32, name="plain", align_bytes=64)
         nc.vector.tensor_copy(out=plain[:], in_=zq2[1][:].rearrange(flat))
         s1 = add("s1", [P, 2, HALF], sq1[:, 1], sq2[:, 1])
-        half_root(0, s0)
+        send_half(nc.sync, 0, root("wide0", s0, [P, 2, HALF]))
         nc.vector.tensor_tensor(out=sqq2[:, 1], in0=zq2[1][:].rearrange(flat), in1=plain[:], op=ALU.mult)
         for g in range(G):
             nc.scalar.activation(out=sqq3[:, g], in_=zq3[g][:].rearrange(flat), func=ACT.Square)
-        half_root(1, s1)
+        wide1 = root("wide1", s1, [P, 2, HALF])
         s2 = add("s2", [P, G, 2 * COLS], sqq2[:, :, 0, :], sqq2[:, :, 1, :])
         s3 = add("s3", [P, G, 2 * COLS], sqq3[:, :, 0, :], sqq3[:, :, 1, :])
-        quarter_root(2, mg2, s2)
-        quarter_root(3, mg3, s3)
+        wide2 = root("wide2", s2, [P, G, 2 * COLS])
+        send_half(nc.scalar, 1, wide1)
+        send_quarter(nc.sync, 2, 0, wide2)
+        wide3 = root("wide3", s3, [P, G, 2 * COLS])
+        send_quarter(nc.scalar, 2, 1, wide2)
+        for g in range(G):
+            send_quarter(nc.sync, 3, g, wide3)
         warm_gate = sb.tile([P, 1], F32, name="warm_gate")
         nc.scalar.activation(out=warm_gate[:], in_=one[:], func=ACT.Sigmoid)
 
@@ -182,21 +184,29 @@ def tile_rows_fmagnitude_kernel(tc, x, w1, w2, th, hs, wo2, ob, osc, out):
         nc.vector.transpose(out=columns[:].rearrange("p a k i -> p (a k i)"), in_=runs[:].rearrange("p a k i -> p (a k i)"))
         woq = prepare("wo", halves(wo_raw), nc.vector.tensor_copy)
 
-        quarters = N // COLS
         sig = [sb.tile([P, PACK, COLS], F32, name="sig%d" % q, align_bytes=64) for q in range(quarters)]
-        hidden = [sb.tile([P, PACK, COLS], BF16, name="hidden%d" % q, align_bytes=64) for q in range(quarters)]
+        scaled = [sb.tile([P, PACK, COLS], F32, name="scaled%d" % q, align_bytes=64) for q in range(quarters)]
         bent = [sb.tile([P, 4, COLS], F32, name="bent%d" % q, align_bytes=64) for q in range(quarters)]
         res = [sb.tile([P, 4, COLS], F32, name="res%d" % q, align_bytes=64) for q in range(quarters)]
         hh = {}
         y = {}
 
-        def gate(q, j):
-            nc.scalar.activation(out=sig[q][:, j, :], in_=mg[q][:, j, :], func=ACT.Sigmoid, bias=neg_th[:, j : j + 1])
-            nc.vector.scalar_tensor_tensor(out=hidden[q][:, j, :], in0=mg[q][:, j, :], scalar=hs_sb[:, j : j + 1],
-                                           in1=sig[q][:, j, :], op0=ALU.mult, op1=ALU.mult)
+        def scale(q):
+            for j in range(PACK):
+                nc.vector.tensor_scalar(out=scaled[q][:, j, :], in0=mg[q][:, j, :], scalar1=hs_sb[:, j : j + 1],
+                                        scalar2=None, op0=ALU.mult)
 
-        def pack(q):
-            hh.setdefault(q, interleave(nc.vector.tensor_copy, "hh%d" % q, hidden[q][:]))
+        def gate(q):
+            for j in range(PACK):
+                nc.scalar.activation(out=sig[q][:, j, :], in_=mg[q][:, j, :], func=ACT.Sigmoid, bias=neg_th[:, j : j + 1])
+            hidden = words("hh%d" % q, COLS)
+            nc.vector.tensor_tensor(
+                out=hidden[:].rearrange("p (c i j) -> p c j i", i=2, j=PACK),
+                in0=scaled[q][:].rearrange("p j (c i) -> p c j i", i=2),
+                in1=sig[q][:].rearrange("p j (c i) -> p c j i", i=2),
+                op=ALU.mult,
+            )
+            hh.setdefault(q, hidden)
 
         def second_layer(q):
             moving = quantize("hq%d" % q, hh[q])
@@ -220,25 +230,26 @@ def tile_rows_fmagnitude_kernel(tc, x, w1, w2, th, hs, wo2, ob, osc, out):
         def store(q, first, last):
             nc.sync.dma_start(out=out_v[:, first:last, COLS * q : COLS * q + COLS], in_=res[q][:, first:last, :])
 
-        for j in range(PACK):
-            gate(0, j)
-        for q in range(1, quarters):
-            gate(q, 0)
-            pack(q - 1)
-            gate(q, 1)
-            gate(q, 2)
-            second_layer(q - 1)
-            gate(q, 3)
+        scale(0)
+        scale(1)
+        gate(0)
+        scale(2)
+        second_layer(0)
+        gate(1)
+        second_layer(1)
+        gate(2)
+        scale(3)
+        second_layer(2)
+        gate(3)
         bend(0)
         for k in range(4):
             nc.scalar.activation(out=res[0][:, k, :], in_=bent[0][:, k, :], func=ACT.Copy, scale=columns[:, 1, k, 0:1])
         store(0, 0, 4)
         bend(1)
         factor(1, 0)
-        pack(3)
         factor(1, 1)
-        factor(1, 2)
         second_layer(3)
+        factor(1, 2)
         factor(1, 3)
         store(1, 0, 4)
         bend(2)

from contextlib import ExitStack

import concourse.mybir as mybir

G, D, M, O, N = 2, 256, 256, 256, 512
FLOPS = 2 * G * N * (2 * D * M + M * O)

F32 = mybir.dt.float32
BF16 = mybir.dt.bfloat16
U32 = mybir.dt.uint32
U8 = mybir.dt.uint8
FP8X4 = mybir.dt.float8_e4m3fn_x4
ACT = mybir.ActivationFunctionType
ALU = mybir.AluOpType

P = 128
R = 64
PACK = 4
HALF = 256
COLS = 128
FLOOR = 0.05


def tile_rows_fmagnitude_kernel(tc, x, w1, w2, th, hs, wo2, ob, osc, out):
    nc = tc.nc
    with ExitStack() as ctx:
        sb = ctx.enter_context(tc.tile_pool(name="sb", bufs=1))
        ps = ctx.enter_context(tc.psum_pool(name="ps", bufs=1))
        ctx.enter_context(tc.manual_schedule())

        def rows(g):
            return slice(R * g, R * g + R)

        def load(name, src, width):
            raw = sb.tile([P, PACK, width], F32, name=name, align_bytes=64)
            nc.sync.dma_start(out=raw[:], in_=src)
            return raw

        by_word = "g (p j) c -> (g p) j c"
        xv = x.rearrange(by_word, j=PACK)
        x_raw0 = load("x_raw0", xv[:, :, 0:HALF], HALF)
        w1_raw = load("w1_raw", w1.rearrange(by_word, j=PACK), M)

        one = sb.tile([P, 1], F32, name="one")
        nc.vector.memset(one[:], 1.0)
        runs = sb.tile([P, 2, 4, 32], F32, name="runs", align_bytes=64)
        nc.vector.memset(runs[:], 0.0)
        warm = sb.tile([P, 1], F32, name="warm")
        nc.scalar.activation(out=warm[:], in_=one[:], func=ACT.Sqrt)

        w2_raw = load("w2_raw", w2.rearrange(by_word, j=PACK), M)
        x_raw1 = load("x_raw1", xv[:, :, HALF:N], HALF)
        wo_raw = load("wo_raw", wo2.rearrange(by_word, j=PACK), O)

        th_sb = sb.tile([P, PACK], F32, name="th_sb")
        nc.sync.dma_start(out=th_sb[:], in_=th.rearrange("g (p j) c -> (g p) (j c)", j=PACK))
        hs_sb = sb.tile([P, PACK], F32, name="hs_sb")
        nc.sync.dma_start(out=hs_sb[:], in_=hs.rearrange("g (p j) c -> (g p) (j c)", j=PACK))
        by_run = "g (t b i) c -> b (g t) (i c)"
        nc.sync.dma_start(out=runs[0:P:32, 0], in_=ob.rearrange(by_run, t=2, b=4))
        nc.sync.dma_start(out=runs[0:P:32, 1], in_=osc.rearrange(by_run, t=2, b=4))

        def words(name, width):
            return sb.tile([P, width * PACK], BF16, name=name, align_bytes=64)

        def interleave(copy, name, columns_in):
            dst = words(name, COLS)
            copy(
                out=dst[:].rearrange("p (c i j) -> p c j i", i=4, j=PACK),
                in_=columns_in.rearrange("p j (c i) -> p c j i", i=4),
            )
            return dst

        def halves(raw):
            return raw[:, :, 0:COLS], raw[:, :, COLS : 2 * COLS]

        def dealt(raw):
            return raw[:, :, 0:M:2], raw[:, :, 1:M:2]

        def quantize(name, src):
            codes = sb.tile([P, COLS], U32, name=name + "_codes", align_bytes=64)
            scales = sb.tile([P, COLS], U8, name=name + "_scales", align_bytes=64)
            nc.vector.quantize_mx(out=codes[:].bitcast(FP8X4), scales=scales[:], in_=src[:])
            return codes, scales

        def prepare(name, parts, second_copy):
            first = interleave(nc.vector.tensor_copy, name + "_il0", parts[0])
            second = interleave(second_copy, name + "_il1", parts[1])
            return [quantize(name + "0", first), quantize(name + "1", second)]

        def product(dst, g, weights, moving):
            nc.tensor.matmul_mx(
                out=dst,
                lhsT=weights[0][rows(g)].bitcast(FP8X4),
                lhsT_scale=weights[1][rows(g)],
                rhs=moving[0][rows(g)].bitcast(FP8X4),
                rhs_scale=moving[1][rows(g)],
                start=True,
                stop=True,
            )

        def half_products(w, wq, xq):
            banks = [ps.tile([P, 2, HALF], F32, name="z", tag="bank%d%d" % (g, w)) for g in range(G)]
            for t, order in ((0, ((0, 0), (1, 0), (0, 1), (1, 1))), (1, ((0, 0), (0, 1), (1, 0), (1, 1)))):
                for g, e in order:
                    product(banks[g][:, t, COLS * e : COLS * e + COLS], g, wq[t], xq[e])
            return banks

        def quarter_products(q, moving):
            banks = [ps.tile([P, 2, 2, COLS], F32, name="z", tag="bank%d%d" % (g, q)) for g in range(G)]
            for g in range(G):
                for w, wq in enumerate((w1q, w2q)):
                    for t in range(2):
                        product(banks[g][:, w, t, :], g, wq[t], moving)
            return banks

        def square(dst, bank):
            nc.scalar.activation(out=dst, in_=bank[:], func=ACT.Square)

        def add(name, shape, a, b):
            total = sb.tile(shape, F32, name=name, align_bytes=64)
            nc.vector.tensor_tensor(out=total[:], in0=a, in1=b, op=ALU.add)
            return total

        def root(name, total, shape):
            wide = sb.tile(shape, F32, name=name, align_bytes=64)
            nc.scalar.activation(out=wide[:], in_=total[:], func=ACT.Sqrt, bias=FLOOR)
            return wide

        xq = prepare("x0", halves(x_raw0), nc.vector.tensor_copy)
        w1q = prepare("w1", dealt(w1_raw), nc.scalar.copy)
        z1 = half_products(0, w1q, xq)
        w2q = prepare("w2", dealt(w2_raw), nc.vector.tensor_copy)
        z2 = half_products(1, w2q, xq)
        xq1 = prepare("x1", halves(x_raw1), nc.vector.tensor_copy)
        zq2 = quarter_products(2, xq1[0])
        zq3 = quarter_products(3, xq1[1])

        quarters = N // COLS
        mg = [sb.tile([P, PACK, COLS], F32, name="mg%d" % q, align_bytes=64) for q in range(quarters)]

        sq1 = sb.tile([P, G, 2, HALF], F32, name="sq1", align_bytes=64)
        sq2 = sb.tile([P, G, 2, HALF], F32, name="sq2", align_bytes=64)
        sqq2 = sb.tile([P, G, 2, 2 * COLS], F32, name="sqq2", align_bytes=64)
        sqq3 = sb.tile([P, G, 2, 2 * COLS], F32, name="sqq3", align_bytes=64)
        flat = "p w t n -> p w (t n)"

        def send_half(queue, g, wide):
            for q in range(2):
                queue.dma_start(out=mg[q][rows(g)], in_=wide[:, :, COLS * q : COLS * q + COLS])

        def send_quarter(queue, q, g, wide):
            queue.dma_start(out=mg[q][rows(g)], in_=wide[:, g, :])

        square(sq1[:, 0], z1[0])
        square(sq1[:, 1], z1[1])
        square(sq2[:, 0], z2[0])
        s0 = add("s0", [P, 2, HALF], sq1[:, 0], sq2[:, 0])
        square(sq2[:, 1], z2[1])
        nc.scalar.activation(out=sqq2[:, 0], in_=zq2[0][:].rearrange(flat), func=ACT.Square)
        plain = sb.tile([P, 2, 2 * COLS], F32, name="plain", align_bytes=64)
        nc.vector.tensor_copy(out=plain[:], in_=zq2[1][:].rearrange(flat))
        s1 = add("s1", [P, 2, HALF], sq1[:, 1], sq2[:, 1])
        send_half(nc.sync, 0, root("wide0", s0, [P, 2, HALF]))
        nc.vector.tensor_tensor(out=sqq2[:, 1], in0=zq2[1][:].rearrange(flat), in1=plain[:], op=ALU.mult)
        for g in range(G):
            nc.scalar.activation(out=sqq3[:, g], in_=zq3[g][:].rearrange(flat), func=ACT.Square)
        wide1 = root("wide1", s1, [P, 2, HALF])
        s2 = add("s2", [P, G, 2 * COLS], sqq2[:, :, 0, :], sqq2[:, :, 1, :])
        s3 = add("s3", [P, G, 2 * COLS], sqq3[:, :, 0, :], sqq3[:, :, 1, :])
        wide2 = root("wide2", s2, [P, G, 2 * COLS])
        send_half(nc.scalar, 1, wide1)
        send_quarter(nc.sync, 2, 0, wide2)
        wide3 = root("wide3", s3, [P, G, 2 * COLS])
        send_quarter(nc.scalar, 2, 1, wide2)
        for g in range(G):
            send_quarter(nc.sync, 3, g, wide3)
        warm_gate = sb.tile([P, 1], F32, name="warm_gate")
        nc.scalar.activation(out=warm_gate[:], in_=one[:], func=ACT.Sigmoid)

        neg_th = sb.tile([P, PACK], F32, name="neg_th")
        nc.vector.tensor_scalar(out=neg_th[:], in0=th_sb[:], scalar1=-1.0, scalar2=None, op0=ALU.mult)
        columns = sb.tile([P, 2, 4, 32], F32, name="columns", align_bytes=64)
        nc.vector.transpose(out=columns[:].rearrange("p a k i -> p (a k i)"), in_=runs[:].rearrange("p a k i -> p (a k i)"))
        woq = prepare("wo", halves(wo_raw), nc.vector.tensor_copy)

        sig = [sb.tile([P, PACK, COLS], F32, name="sig%d" % q, align_bytes=64) for q in range(quarters)]
        scaled = [sb.tile([P, PACK, COLS], F32, name="scaled%d" % q, align_bytes=64) for q in range(quarters)]
        bent = [sb.tile([P, 4, COLS], F32, name="bent%d" % q, align_bytes=64) for q in range(quarters)]
        res = [sb.tile([P, 4, COLS], F32, name="res%d" % q, align_bytes=64) for q in range(quarters)]
        hh = {}
        y = {}

        def scale(q):
            for j in range(PACK):
                nc.vector.tensor_scalar(out=scaled[q][:, j, :], in0=mg[q][:, j, :], scalar1=hs_sb[:, j : j + 1],
                                        scalar2=None, op0=ALU.mult)

        def gate(q):
            for j in range(PACK):
                nc.scalar.activation(out=sig[q][:, j, :], in_=mg[q][:, j, :], func=ACT.Sigmoid, bias=neg_th[:, j : j + 1])
            hidden = words("hh%d" % q, COLS)
            nc.vector.tensor_tensor(
                out=hidden[:].rearrange("p (c i j) -> p c j i", i=2, j=PACK),
                in0=scaled[q][:].rearrange("p j (c i) -> p c j i", i=2),
                in1=sig[q][:].rearrange("p j (c i) -> p c j i", i=2),
                op=ALU.mult,
            )
            hh.setdefault(q, hidden)

        def second_layer(q):
            moving = quantize("hq%d" % q, hh[q])
            banks = [ps.tile([P, 2, COLS], F32, name="y", tag="bank%d%d" % (g, q)) for g in range(G)]
            for g in range(G):
                for t in range(2):
                    product(banks[g][:, t, :], g, woq[t], moving)
            y.setdefault(q, banks)

        out_v = out.rearrange("g (t q) n -> q (g t) n", q=P)

        def bend(q):
            for k in range(4):
                nc.scalar.activation(out=bent[q][:, k, :], in_=y[q][k // 2][:, k % 2, :], func=ACT.Tanh,
                                     bias=columns[:, 0, k, 0:1])

        def factor(q, k):
            nc.vector.tensor_scalar(out=res[q][:, k, :], in0=bent[q][:, k, :], scalar1=columns[:, 1, k, 0:1], scalar2=None,
                                    op0=ALU.mult)

        def store(q, first, last):
            nc.sync.dma_start(out=out_v[:, first:last, COLS * q : COLS * q + COLS], in_=res[q][:, first:last, :])

        scale(0)
        scale(1)
        gate(0)
        scale(2)
        second_layer(0)
        gate(1)
        second_layer(1)
        gate(2)
        scale(3)
        second_layer(2)
        gate(3)
        bend(0)
        for k in range(4):
            nc.scalar.activation(out=res[0][:, k, :], in_=bent[0][:, k, :], func=ACT.Copy, scale=columns[:, 1, k, 0:1])
        store(0, 0, 4)
        bend(1)
        factor(1, 0)
        factor(1, 1)
        second_layer(3)
        factor(1, 2)
        factor(1, 3)
        store(1, 0, 4)
        bend(2)
        for k in range(4):
            factor(2, k)
        store(2, 0, 4)
        bend(3)
        for g in range(G):
            factor(3, 2 * g)
            factor(3, 2 * g + 1)
            store(3, 2 * g, 2 * g + 2)
